import numpy as np
CORES = [34,42,162,170,290,298,418,426]
N = 8
ROOT = 2
def setup_inputs(rng):
    return {"x": rng.standard_normal((N, 128, 8), dtype=np.float32)}
def reference(x):
    y = np.full((N, 128, N * 8), np.nan, x.dtype)
    y[ROOT] = np.concatenate(list(x), axis=1)
    return {"y": y}

@@ -1,0 +1,57 @@
+SCRATCH = {
+    "stage": ("dram", [128, 8], "float32"),
+    "land": ("sbuf", [128, 64], "float32"),
+}
+SEMAPHORES = ["loaded", "sent", "arrived", "stored"]
+
+W = 8
+ENGINES = 8
+
+
+def core_at(host, chip, core):
+    return host * 128 + chip * 8 + core
+
+
+def relay_of(src, root, topo):
+    if topo.may_write(src, root):
+        return None
+    if topo.chip(src) == topo.chip(root):
+        return core_at(topo.host(src) ^ 1, topo.chip(src), 3)
+    return core_at(topo.host(root) ^ 1, topo.chip(src), 3)
+
+
+def send(g, T, topo, core, dst, out_ap):
+    rid, pid = topo.addr(dst, core)
+    g.remote_dma(out_ap, T.stage[:], T.sem.arrived, T.sem.sent, pid, rid, topo.mask(core, dst))
+    g.wait_ge(T.sem.sent, ENGINES)
+
+
+def rank_program(g, core, T, topo):
+    root = T.cores[2]
+    relays = {relay_of(c, root, topo): j for j, c in enumerate(T.cores) if c != root}
+    relays.pop(None, None)
+    rank = T.rank_of(core)
+
+    if core in relays:
+        j = relays[core]
+        g.wait_ge(T.sem.arrived, ENGINES)
+        send(g, T, topo, core, root, T.land[:, W * j:W * (j + 1)])
+        return
+    if rank is None:
+        return
+
+    if core == root:
+        g.dma_start(T.land[:, W * rank:W * (rank + 1)], T.x[:]).then_inc(T.sem.loaded, 16)
+        g.wait_ge(T.sem.loaded, 16)
+        g.wait_ge(T.sem.arrived, ENGINES * (len(T.cores) - 1))
+        g.dma_start(T.y[:], T.land[:]).then_inc(T.sem.stored, 16)
+        g.wait_ge(T.sem.stored, 16)
+        return
+
+    g.dma_start(T.stage[:], T.x[:]).then_inc(T.sem.loaded, 16)
+    g.wait_ge(T.sem.loaded, 16)
+    relay = relay_of(core, root, topo)
+    if relay is None:
+        send(g, T, topo, core, root, T.land[:, W * rank:W * (rank + 1)])
+    else:
+        send(g, T, topo, core, relay, T.stage[:])

@@ -16,8 +16,8 @@ def relay_of(src, root, topo):
     if topo.may_write(src, root):
         return None
     if topo.chip(src) == topo.chip(root):
-        return core_at(topo.host(src) ^ 1, topo.chip(src), 3)
-    return core_at(topo.host(root) ^ 1, topo.chip(src), 3)
+        return core_at(topo.host(root) ^ 1, topo.chip(root), 3)
+    return core_at(topo.host(src) ^ 1, topo.chip(root), 3)
 
 
 def send(g, T, topo, core, dst, out_ap):

SCRATCH = {
    "stage": ("dram", [128, 8], "float32"),
    "land": ("sbuf", [128, 64], "float32"),
}
SEMAPHORES = ["loaded", "sent", "arrived", "stored"]

W = 8
ENGINES = 8


def core_at(host, chip, core):
    return host * 128 + chip * 8 + core


def relay_of(src, root, topo):
    if topo.may_write(src, root):
        return None
    if topo.chip(src) == topo.chip(root):
        return core_at(topo.host(root) ^ 1, topo.chip(root), 3)
    return core_at(topo.host(src) ^ 1, topo.chip(root), 3)


def send(g, T, topo, core, dst, out_ap):
    rid, pid = topo.addr(dst, core)
    g.remote_dma(out_ap, T.stage[:], T.sem.arrived, T.sem.sent, pid, rid, topo.mask(core, dst))
    g.wait_ge(T.sem.sent, ENGINES)


def rank_program(g, core, T, topo):
    root = T.cores[2]
    relays = {relay_of(c, root, topo): j for j, c in enumerate(T.cores) if c != root}
    relays.pop(None, None)
    rank = T.rank_of(core)

    if core in relays:
        j = relays[core]
        g.wait_ge(T.sem.arrived, ENGINES)
        send(g, T, topo, core, root, T.land[:, W * j:W * (j + 1)])
        return
    if rank is None:
        return

    if core == root:
        g.dma_start(T.land[:, W * rank:W * (rank + 1)], T.x[:]).then_inc(T.sem.loaded, 16)
        g.wait_ge(T.sem.loaded, 16)
        g.wait_ge(T.sem.arrived, ENGINES * (len(T.cores) - 1))
        g.dma_start(T.y[:], T.land[:]).then_inc(T.sem.stored, 16)
        g.wait_ge(T.sem.stored, 16)
        return

    g.dma_start(T.stage[:], T.x[:]).then_inc(T.sem.loaded, 16)
    g.wait_ge(T.sem.loaded, 16)
    relay = relay_of(core, root, topo)
    if relay is None:
        send(g, T, topo, core, root, T.land[:, W * rank:W * (rank + 1)])
    else:
        send(g, T, topo, core, relay, T.stage[:])
